import numpy as np, ml_dtypes
CORES = [1,129,9,137,57,185,105,233,113,241,121,249]
N = 12
QP = 64
def setup_inputs(rng):
    return {"q": rng.standard_normal((N, 128, QP), dtype=np.float32).astype(ml_dtypes.bfloat16), "k": rng.standard_normal((N, 128, 128), dtype=np.float32).astype(ml_dtypes.bfloat16), "v": rng.standard_normal((N, 128, 128), dtype=np.float32).astype(ml_dtypes.bfloat16), "b": (8 * rng.standard_normal((N, 128, N * QP), dtype=np.float32)).astype(ml_dtypes.bfloat16)}
def setup_inputs_big(rng):
    d = setup_inputs(rng)
    for k in ("q", "k", "v", "b"): d[k] = (d[k].astype(np.float32) * 1024.0).astype(d[k].dtype)
    return d
def setup_inputs_small(rng):
    d = setup_inputs(rng)
    for k in ("q", "k", "v", "b"): d[k] = (d[k].astype(np.float32) * (1 / 1024.0)).astype(d[k].dtype)
    return d
def setup_inputs_apart(rng):
    d = setup_inputs(rng)
    f = (10.0 ** rng.permutation(np.linspace(-1.5, 1.5, N))).astype(np.float32).reshape(N, 1, 1)
    for k in ("q", "k", "v", "b"): d[k] = (d[k].astype(np.float32) * f).astype(d[k].dtype)
    return d
def reference(q, k, v, b):
    Q, K, V, B = q.astype(np.float64), k.astype(np.float64), v.astype(np.float64), b.astype(np.float64)
    y = np.zeros((N, 128, QP))
    for r in range(N):
        for j in range(N):
            y[r] += V[j].T @ np.maximum(K[j].T @ Q[r] + B[r][:, QP * j:QP * j + QP], 0.0)
    return {"y": y.astype(ml_dtypes.bfloat16 if q.dtype != np.float64 else np.float64)}

from concourse.bass import DstId, RemoteDMATransfer
from concourse.mybir import AluOpType

N = 12
QP = 64
KP = 128
SLOT = 2 * KP
NSIM = 256
NBANK = 6

D_OWN = 4
PER_HELPER = 2

SCRATCH = {
    "kv": ("sbuf", [128, N * SLOT], "bfloat16"),
    "qs": ("sbuf", [128, QP], "bfloat16"),
    "bs": ("sbuf", [128, N * QP], "bfloat16"),
    "nb": ("sbuf", [128, N * QP], "bfloat16"),
    "zero": ("sbuf", [128, N * QP], "bfloat16"),
    "mx": ("sbuf", [128, N * QP], "bfloat16"),
    "ys": ("sbuf", [128, QP], "bfloat16"),
    "po": ("psum", [128, 512], "float32"),
}
for _i in range(NBANK):
    SCRATCH["ps%d" % _i] = ("psum", [128, 512], "float32")

SEMAPHORES = ["ldkv", "ldq", "ldb", "sent", "zs", "ns", "ss", "ms", "oacc", "yr", "st"] + ["a%d" % _i for _i in range(N)]

_CACHE = {}


def _bits(mask):
    return [i for i in range(16) if (mask >> i) & 1]


def _mask(bits):
    m = 0
    for b in bits:
        m |= 1 << b
    return m


def _chunks(lst, k):
    return [lst[i:i + k] for i in range(0, len(lst), k)]


def _plan(cores, topo):
    n = len(cores)
    jobs, need, key = {}, {}, {}
    for s, c in enumerate(cores):
        chipc = [x for x in range(NSIM) if x != c and topo.host(x) == topo.host(c) and topo.chip(x) == topo.chip(c)]
        plane = [r for r in range(n) if r == s or topo.may_write(c, cores[r])]
        cross = [r for r in range(n) if r not in plane]
        i = plane.index(s)
        owners = [h for h in chipc if all(topo.may_write(h, cores[r]) for r in cross)]
        pool = {}
        for side in (0, 1):
            on_side = [h for h in chipc if (topo.die(h) != topo.die(c)) == bool(side)]
            pool[side] = [h for h in on_side if h in owners] + [h for h in on_side if h not in owners]
        rot = [plane[(i + t) % len(plane)] for t in range(1, len(plane))]
        direct, rest = rot[:D_OWN], rot[D_OWN:]
        lists = []
        for side in (0, 1):
            xs = [r for jx, r in enumerate(cross) if (i + jx) % 2 == side]
            sh = (i // 2) % max(1, len(xs))
            xs = xs[sh:] + xs[:sh]
            part = _chunks(xs, PER_HELPER)
            more = rest[:1] if side == 0 else rest[1:]
            part = part + _chunks(more, PER_HELPER)
            for h, lst in zip(pool[side], part):
                lists.append((h, lst))
        lists.sort(key=lambda e: -len(e[1]))
        calls = []
        off = _bits(topo.mask(c, cores[direct[0]]))
        if lists:
            on = [b for b in _bits(topo.mask(c, lists[0][0])) if b not in off]
            calls.append([(_mask(on), [h for h, _ in lists])])
            for hi, (h, lst) in enumerate(lists):
                need[(h, s)] = len(on)
                hb = _bits(topo.mask(h, cores[lst[0]]))
                jobs.setdefault(h, []).append((s, len(on), [[(_mask(hb), [cores[r] for r in lst])]]))
                for p, r in enumerate(lst):
                    need[(cores[r], s)] = len(hb)
                    key[(r, s)] = (1, hi + p, s)
        calls.append([(_mask(off), [cores[r] for r in direct])])
        for p, r in enumerate(direct):
            need[(cores[r], s)] = len(off)
            key[(r, s)] = (0, p, s)
        jobs.setdefault(c, []).append((s, None, calls))
    return jobs, need, key


def rank_program(g, core, T, topo):
    cores = list(T.cores)
    if "plan" not in _CACHE:
        _CACHE["plan"] = _plan(cores, topo)
    jobs, need, key = _CACHE["plan"]
    rank = T.rank_of(core)
    sem = T.sem

    def slot(j):
        return T.kv[:, SLOT * j:SLOT * (j + 1)]

    if rank is not None:
        g.sync.dma_start(T.kv[:, SLOT * rank:SLOT * rank + KP], T.k[:]).then_inc(sem.ldkv, 16)
        g.scalar.dma_start(T.kv[:, SLOT * rank + KP:SLOT * (rank + 1)], T.v[:]).then_inc(sem.ldkv, 16)
        g.sync.dma_start(T.qs[:], T.q[:]).then_inc(sem.ldq, 16)
        g.scalar.dma_start(T.bs[:], T.b[:]).then_inc(sem.ldb, 16)

    sent = 0
    for s, cnt, calls in jobs.get(core, []):
        if cnt is None:
            g.wait_ge(sem.ldkv, 32)
        else:
            g.wait_ge(sem["a%d" % s], cnt)
        for call in calls:
            trs = []
            for m, dsts in call:
                ids = []
                for d in dsts:
                    rid, pid = topo.addr(d, core)
                    ids.append(DstId(rid=rid, pnc=pid))
                trs.append(RemoteDMATransfer(dst_ids=ids, dma_engine_mask=m, remote_sem=sem["a%d" % s],
                                             srcs=[slot(s)], dsts=[slot(s) for _ in dsts], alu_op=0))
                sent += len(_bits(m))
            g.remote_dma_fused(trs, local_sem=sem.sent)
    if sent:
        g.wait_ge(sem.sent, sent)
    if rank is None:
        return

    order = [rank] + sorted([j for j in range(N) if j != rank], key=lambda j: key[(rank, j)])

    def kk(j):
        return T.kv[:, SLOT * j:SLOT * j + KP]

    def vv(j):
        return T.kv[:, SLOT * j + KP:SLOT * (j + 1)]

    def cols(t, j):
        return t[:, QP * j:QP * (j + 1)]

    acc = T.po[:, 0:QP]
    te, ve = g.tensor, g.vector

    te.wait_ge(sem.ldq, 16)
    te.wait_ge(sem.ldb, 16)
    for p, j in enumerate(order):
        if j == rank:
            te.wait_ge(sem.ldkv, 32)
        else:
            te.wait_ge(sem["a%d" % j], need[(core, j)])
        te.matmul(T["ps%d" % (p % NBANK)][:, 0:QP], kk(j), T.qs[:], True, True).then_inc(sem.ss, 1)
        te.matmul(acc, vv(j), cols(T.bs, j), p == 0, False).then_inc(sem.oacc, 1)
        if p >= 1:
            te.wait_ge(sem.ms, p)
            te.matmul(acc, vv(order[p - 1]), cols(T.mx, order[p - 1]), False, False).then_inc(sem.oacc, 1)
    te.wait_ge(sem.ms, N)
    te.matmul(acc, vv(order[-1]), cols(T.mx, order[-1]), False, True).then_inc(sem.oacc, 1)

    ve.memset(T.zero[:], 0.0).then_inc(sem.zs, 1)
    ve.wait_ge(sem.zs, 1)
    ve.wait_ge(sem.ldb, 16)
    ve.tensor_tensor(T.nb[:], T.zero[:], T.bs[:], AluOpType.subtract).then_inc(sem.ns, 1)
    ve.wait_ge(sem.ns, 1)
    for p, j in enumerate(order):
        ve.wait_ge(sem.ss, p + 1)
        ve.tensor_tensor(cols(T.mx, j), T["ps%d" % (p % NBANK)][:, 0:QP], cols(T.nb, j), AluOpType.max).then_inc(sem.ms, 1)
    ve.wait_ge(sem.oacc, 2 * N)
    ve.tensor_copy(T.ys[:], acc).then_inc(sem.yr, 1)

    g.sync.wait_ge(sem.yr, 1)
    g.sync.dma_start(T.y[:], T.ys[:]).then_inc(sem.st, 16)
    g.sync.wait_ge(sem.st, 16)
